import numpy as np
import ml_dtypes


def mxq(x, axis, fmt="e4m3"):
    dtype, down = {"e4m3": (ml_dtypes.float8_e4m3fn, 7), "e5m2": (ml_dtypes.float8_e5m2, 14)}[fmt]
    v = np.moveaxis(np.asarray(x, np.float32).astype(ml_dtypes.bfloat16).astype(np.float64), axis, -1)
    blocks = v.reshape(v.shape[:-1] + (-1, 32))
    amax = np.abs(blocks).max(-1, keepdims=True)
    byte = np.maximum(np.where(amax > 0, np.frexp(amax)[1] - 1 + 127, 0) - down, 1)
    scale = np.exp2(byte - 127.0)
    codes = (blocks / scale).astype(np.float32).astype(dtype).astype(np.float64)
    return np.moveaxis((codes * scale).reshape(v.shape), -1, axis)


WIDE = False


def mx_kscale(k):
    if not WIDE:
        return np.ones(k)
    levels = np.array([30, -30])
    if k % 512:
        return np.exp2(np.random.permutation(np.resize(levels, k // 32))).repeat(32)
    a = np.empty((k // 512, 16))
    for p in range(k // 512):
        a[p, :8] = np.random.permutation(np.resize(levels, 8))
        for g in range(8):
            far = levels[np.abs(levels - a[p, g]) >= 10]
            a[p, g + 8] = far[np.random.randint(len(far))]
    return np.exp2(a.ravel()).repeat(32)


def f64(x):
    return np.asarray(x).astype(np.float64)


def striped(idx):
    return np.tile(np.asarray(idx).reshape(-1, 16).T, (8, 1)).astype(np.uint16)


def unstriped(offs):
    return offs[:16].T.reshape(-1).astype(np.int64)


E2M1 = np.array([0.0, 0.5, 1.0, 1.5, 2.0, 3.0, 4.0, 6.0, -0.0, -0.5, -1.0, -1.5, -2.0, -3.0, -4.0, -6.0])


def pack_weight(w, fmt):
    k, n = w.shape
    w = f64(np.asarray(w, np.float32).astype(ml_dtypes.bfloat16)).reshape(k // 32, 32, n)
    amax = np.abs(w).max(1)
    if fmt in ("e4m3", "e5m2"):
        byte = np.frexp(amax)[1] - 1 + 127 - (7 if fmt == "e4m3" else 14)
    else:
        mant, ex = np.frexp(amax / 6.0)
        byte = np.where(mant > 0.5, ex, ex - 1) + 127
    byte = np.clip(np.where(amax > 0, byte, 1), 1, 254)
    scaled = (w * np.exp2(127.0 - byte)[:, None, :]).reshape(k, n).astype(np.float32)
    by_word = np.ascontiguousarray(scaled.reshape(k // 512, 128, 4, n).transpose(0, 1, 3, 2))
    if fmt in ("e4m3", "e5m2"):
        words = by_word.astype(ml_dtypes.float8_e4m3fn if fmt == "e4m3" else ml_dtypes.float8_e5m2).view(np.uint8)
    else:
        c = by_word.astype(ml_dtypes.float4_e2m1fn).view(np.uint8) & 0xF
        words = (c[..., 0::2] | (c[..., 1::2] << 4)).reshape(k // 512, 128, 2 * n)
    return np.ascontiguousarray(words), np.ascontiguousarray(byte.astype(np.uint8).reshape(k // 512, 16, n))


def unpack_weight(words, scales, fmt):
    g, _, n = scales.shape
    words = np.ascontiguousarray(words).reshape(g, 128, n, -1)
    if fmt in ("e4m3", "e5m2"):
        vals = words.view(ml_dtypes.float8_e4m3fn if fmt == "e4m3" else ml_dtypes.float8_e5m2).astype(np.float64)
    else:
        nib = np.empty((g, 128, n, 4), np.uint8)
        nib[..., 0::2] = words & 0xF
        nib[..., 1::2] = words >> 4
        vals = E2M1[nib]
    vals = vals * np.repeat(np.exp2(scales.astype(np.float64) - 127.0), 8, axis=1)[..., None]
    return vals.transpose(0, 1, 3, 2).reshape(g * 512, n)


def sigmoid(v):
    return 1.0 / (1.0 + np.exp(-v))


def sgn(shape):
    return np.random.uniform(0.5, 2.0, shape) * np.where(np.random.standard_normal(shape) < 0, -1.0, 1.0)


K, T, J, R, F, Z, N, O = 512, 1024, 256, 512, 512, 1024, 256, 128


def setup_inputs():
    n = np.random.standard_normal
    idx = np.random.permutation(T)[:J]
    idx2 = np.random.permutation(Z)[:J]
    idx3 = np.random.permutation(J)[:O]
    idx4 = np.random.permutation(J)[:O]
    idx5 = np.random.permutation(J)[:O]
    idx6 = np.random.permutation(J)[:O]
    fk = mx_kscale(K)
    ff = mx_kscale(F)
    fr = mx_kscale(R)
    xtp = pack_weight(n((K, T)) / fk[:, None], "e2m1")
    xop = pack_weight(n((F, Z)) / ff[:, None], "e4m3")
    wp = pack_weight(n((K, R)) * 1 / np.sqrt(K) * fk[:, None] * fr, "e4m3")
    w2p = pack_weight(n((F, R)) * 1 / np.sqrt(F) * ff[:, None] * fr, "e2m1")
    wbp = pack_weight(n((R, N)) * 1 / np.sqrt(R) / fr[:, None], "e2m1")
    wcp = pack_weight(n((R, N)) * 1 / np.sqrt(R) / fr[:, None], "e5m2")
    return {
        "xt_words": xtp[0],
        "xt_scales": xtp[1],
        "xo_words": xop[0],
        "xo_scales": xop[1],
        "w_words": wp[0],
        "w_scales": wp[1],
        "w2_words": w2p[0],
        "w2_scales": w2p[1],
        "wb_words": wbp[0],
        "wb_scales": wbp[1],
        "wc_words": wcp[0],
        "wc_scales": wcp[1],
        "so": (np.random.uniform(0.5, 1.6, (N, 1))).astype(np.float32),
        "sp": (sgn((N, 1))).astype(np.float32),
        "bo": (np.random.uniform(-2.0, 2.0, (N, 1))).astype(np.float32),
        "so2": (np.random.uniform(0.5, 1.6, (N, 1))).astype(np.float32),
        "sp2": (sgn((N, 1))).astype(np.float32),
        "bo2": (np.random.uniform(-2.0, 2.0, (N, 1))).astype(np.float32),
        "offs": striped(idx),
        "offs2": striped(idx2),
        "offs3": striped(idx3),
        "offs4": striped(idx4),
        "offs5": striped(idx5),
        "offs6": striped(idx6),
    }


def reference(xt_words, xt_scales, xo_words, xo_scales, w_words, w_scales, w2_words, w2_scales, wb_words, wb_scales, wc_words, wc_scales, so, sp, bo, so2, sp2, bo2, offs, offs2, offs3, offs4, offs5, offs6):
    idx = unstriped(offs)
    idx2 = unstriped(offs2)
    idx3 = unstriped(offs3)
    idx4 = unstriped(offs4)
    idx5 = unstriped(offs5)
    idx6 = unstriped(offs6)
    xtu = unpack_weight(xt_words, xt_scales, "e2m1")
    xou = unpack_weight(xo_words, xo_scales, "e4m3")
    wu = unpack_weight(w_words, w_scales, "e4m3")
    w2u = unpack_weight(w2_words, w2_scales, "e2m1")
    wbu = unpack_weight(wb_words, wb_scales, "e2m1")
    wcu = unpack_weight(wc_words, wc_scales, "e5m2")
    xtidxg = xtu[:, idx]
    a = wu.T @ xtidxg
    xoidx2g = xou[:, idx2]
    b = w2u.T @ xoidx2g
    hid = np.maximum(a, b)
    hidq = mxq(hid, 0, "e5m2")
    p = wbu.T @ hidq
    q = wcu.T @ hidq
    y = p[:, idx3] * f64(so) * sigmoid(q[:, idx4] * f64(sp) + f64(bo)) - q[:, idx5] * f64(so2) * sigmoid(p[:, idx6] * f64(sp2) + f64(bo2))
    return y

@@ -1,0 +1,190 @@
+from contextlib import ExitStack
+
+import concourse.mybir as mybir
+
+F32 = mybir.dt.float32
+BF16 = mybir.dt.bfloat16
+I32 = mybir.dt.int32
+U32 = mybir.dt.uint32
+U16 = mybir.dt.uint16
+U8 = mybir.dt.uint8
+E4M3 = mybir.dt.float8_e4m3fn_x4
+E5M2 = mybir.dt.float8_e5m2_x4
+E2M1 = mybir.dt.float4_e2m1fn_x4
+ACT = mybir.ActivationFunctionType
+ALU = mybir.AluOpType
+
+P = 128
+K, T, J, R, F, Z, N, O = 512, 1024, 256, 512, 512, 1024, 256, 128
+FLOPS = 2 * K * R * J + 2 * F * R * J + 2 * 2 * R * N * J
+
+
+def tile_list_outcomegatedcross_twotab_kernel(
+    tc, xt_words, xt_scales, xo_words, xo_scales, w_words, w_scales, w2_words, w2_scales,
+    wb_words, wb_scales, wc_words, wc_scales, so, sp, bo, so2, sp2, bo2,
+    offs, offs2, offs3, offs4, offs5, offs6, out,
+):
+    nc = tc.nc
+    with ExitStack() as ctx:
+        sb = ctx.enter_context(tc.tile_pool(name="sb", bufs=1))
+        ps = ctx.enter_context(tc.psum_pool(name="ps", bufs=1))
+
+        def tile(name, shape, dt):
+            return sb.tile(shape, dt, name=name, align_bytes=64)
+
+        def words32(ap):
+            return ap[0].rearrange("p n t -> p (n t)").bitcast(I32)
+
+        def by_quadrant(ap):
+            return ap[0].bitcast(I32).rearrange("(q r) c -> r q c", r=4)
+
+        xts_win = tile("xts_win", [P, T], U8)
+        xos_win = tile("xos_win", [P, Z], U8)
+        w_raw_sc = tile("w_raw_sc", [P, 2 * R], U8)
+        out_sc = tile("out_sc", [P, 2 * N], U8)
+        for t in (xts_win, xos_win, w_raw_sc, out_sc):
+            nc.vector.memset(t[:].bitcast(I32), 0)
+
+        st1 = tile("st1", [4, 4, 2 * R // 4], I32)
+        st2 = tile("st2", [4, 4, 2 * N // 4], I32)
+        xtw = tile("xtw", [P, T], U16)
+        xow = tile("xow", [P, Z], U32)
+        ww = tile("ww", [P, R], U32)
+        w2w = tile("w2w", [P, R], U16)
+        wbw = tile("wbw", [P, N], U16)
+        wcw = tile("wcw", [P, N], U32)
+        l1 = tile("l1", [P, J // 16], U16)
+        l2 = tile("l2", [P, J // 16], U16)
+        l3 = tile("l3", [P, O // 16], U16)
+        l4 = tile("l4", [P, O // 16], U16)
+        l5 = tile("l5", [P, O // 16], U16)
+        l6 = tile("l6", [P, O // 16], U16)
+
+        nc.gpsimd.dma_start(xtw[:].bitcast(I32), xt_words[0].bitcast(I32))
+        nc.gpsimd.dma_start(xow[:].bitcast(I32), words32(xo_words))
+        nc.sync.dma_start(st1[:, :, 0 : R // 4], by_quadrant(w_scales))
+        nc.sync.dma_start(st1[:, :, R // 4 : R // 2], by_quadrant(w2_scales))
+        nc.sync.dma_start(l1[:], offs)
+        nc.sync.dma_start(ww[:].bitcast(I32), words32(w_words))
+        for q in range(4):
+            nc.sync.dma_start(xts_win[32 * q : 32 * q + 4, :].bitcast(I32), xt_scales[0, 4 * q : 4 * q + 4, :].bitcast(I32))
+        nc.sync.dma_start(l2[:], offs2)
+        nc.sync.dma_start(w2w[:].bitcast(I32), w2_words[0].bitcast(I32))
+        for q in range(4):
+            nc.sync.dma_start(xos_win[32 * q : 32 * q + 4, :].bitcast(I32), xo_scales[0, 4 * q : 4 * q + 4, :].bitcast(I32))
+        nc.sync.dma_start(st2[:, :, 0 : N // 4], by_quadrant(wb_scales))
+        nc.sync.dma_start(st2[:, :, N // 4 : N // 2], by_quadrant(wc_scales))
+        nc.sync.dma_start(wbw[:].bitcast(I32), wb_words[0].bitcast(I32))
+        nc.sync.dma_start(wcw[:].bitcast(I32), words32(wc_words))
+        vec = {}
+
+        def load_vec(eng, name, ap):
+            vec[name] = tile("v_" + name, [P, 2], F32)
+            with nc.allow_non_contiguous_dma(reason="one value a partition"):
+                eng.dma_start(vec[name][:], ap.rearrange("(h p) o -> p (h o)", p=P))
+
+        nc.sync.dma_start(l6[:], offs6)
+        load_vec(nc.sync, "sp2", sp2)
+        load_vec(nc.sync, "bo2", bo2)
+        nc.sync.dma_start(l3[:], offs3)
+        nc.sync.dma_start(l4[:], offs4)
+        nc.sync.dma_start(l5[:], offs5)
+        load_vec(nc.gpsimd, "so", so)
+        load_vec(nc.gpsimd, "sp", sp)
+        load_vec(nc.gpsimd, "bo", bo)
+        load_vec(nc.gpsimd, "so2", so2)
+
+        for q in range(4):
+            nc.vector.tensor_copy(w_raw_sc[32 * q : 32 * q + 4, :].bitcast(I32), st1[:, q, :])
+        w_sc = tile("w_sc", [P, 2, 4, P], U8)
+        nc.vector.tensor_copy(w_sc[:], w_raw_sc[:].rearrange("p (w m t) -> p w t m", w=2, t=4))
+
+        xts = tile("xts", [P, J], U8)
+        nc.vector.tensor_copy(xts[:], xts_win[:].indirect(l1[:]))
+        xtg = tile("xtg", [P, J], U16)
+        nc.vector.tensor_copy(xtg[:], xtw[:].indirect(l1[:]))
+        xos = tile("xos", [P, J], U8)
+        nc.vector.tensor_copy(xos[:], xos_win[:].indirect(l2[:]))
+        xog = []
+        for h in range(2):
+            g = tile("xog%d" % h, [P, P], U32)
+            nc.vector.tensor_copy(g[:], xow[:].indirect(l2[:, 8 * h : 8 * h + 8]))
+            xog.append(g)
+
+        wp = tile("wp", [P, R], U32)
+        nc.scalar.copy(wp[:].rearrange("p (t c i) -> p c t i", t=4, i=4), ww[:].rearrange("p (c i t) -> p c t i", t=4, i=4))
+        w2p = tile("w2p", [P, R], U16)
+        nc.scalar.copy(w2p[:].rearrange("p (t m) -> p t m", t=4), w2w[:].rearrange("p (m t) -> p t m", t=4))
+
+        a_sb = []
+        for h in range(2):
+            a_ps = ps.tile([P, 4, P], F32, name="a%d" % h)
+            for t in range(4):
+                nc.tensor.matmul_mx(
+                    out=a_ps[:, t, :],
+                    lhsT=wp[:, t * P : (t + 1) * P].bitcast(E4M3), lhsT_scale=w_sc[:, 0, t, :],
+                    rhs=xtg[:, h * P : (h + 1) * P].bitcast(E2M1), rhs_scale=xts[:, h * P : (h + 1) * P],
+                    start=True, stop=True,
+                )
+            s = tile("a_sb%d" % h, [P, P, 4], F32)
+            nc.scalar.copy(s[:], a_ps[:].rearrange("p t j -> p j t"))
+            a_sb.append(s)
+
+        hid = []
+        for h in range(2):
+            b_ps = ps.tile([P, 4, P], F32, name="b%d" % h)
+            for t in range(4):
+                nc.tensor.matmul_mx(
+                    out=b_ps[:, t, :],
+                    lhsT=w2p[:, t * P : (t + 1) * P].bitcast(E2M1), lhsT_scale=w_sc[:, 1, t, :],
+                    rhs=xog[h][:].bitcast(E4M3), rhs_scale=xos[:, h * P : (h + 1) * P],
+                    start=True, stop=True,
+                )
+            s = tile("hid%d" % h, [P, P, 4], BF16)
+            if h == 0:
+                for q in range(4):
+                    nc.vector.tensor_copy(out_sc[32 * q : 32 * q + 4, :].bitcast(I32), st2[:, q, :])
+            nc.vector.tensor_tensor(s[:], b_ps[:].rearrange("p t j -> p j t"), a_sb[h][:], ALU.max)
+            hid.append(s)
+
+        hq = tile("hq", [P, J], U32)
+        hs = tile("hs", [P, J], U8)
+        for h in range(2):
+            nc.vector.quantize_mx(
+                out=hq[:, h * P : (h + 1) * P].bitcast(E5M2), scales=hs[:, h * P : (h + 1) * P],
+                in_=hid[h][:].rearrange("p j t -> p (j t)"),
+            )
+
+        rows = {}
+        for g in range(2):
+            for name, wt, fmt, c0 in (("p", wbw, E2M1, 0), ("q", wcw, E5M2, N)):
+                acc = ps.tile([P, J], F32, name="%s%d_ps" % (name, g))
+                nc.tensor.matmul_mx(
+                    out=acc[:],
+                    lhsT=wt[:, g * P : (g + 1) * P].bitcast(fmt), lhsT_scale=out_sc[:, c0 + g * P : c0 + (g + 1) * P],
+                    rhs=hq[:].bitcast(E5M2), rhs_scale=hs[:],
+                    start=True, stop=True,
+                )
+                s = tile("%s%d" % (name, g), [P, J], F32)
+                nc.vector.tensor_copy(s[:], acc[:])
+                rows[name, g] = s
+
+        for g in range(2):
+            col = slice(g, g + 1)
+            g2 = tile("g2%d" % g, [P, O], F32)
+            nc.scalar.activation(out=g2[:], in_=rows["p", g][:].indirect(l6[:]), func=ACT.Sigmoid,
+                                 bias=vec["bo2"][:, col], scale=vec["sp2"][:, col])
+            va = tile("va%d" % g, [P, O], F32)
+            nc.scalar.activation(out=va[:], in_=rows["p", g][:].indirect(l3[:]), func=ACT.Copy, scale=vec["so"][:, col])
+            g1 = tile("g1%d" % g, [P, O], F32)
+            nc.scalar.activation(out=g1[:], in_=rows["q", g][:].indirect(l4[:]), func=ACT.Sigmoid,
+                                 bias=vec["bo"][:, col], scale=vec["sp"][:, col])
+            vb = tile("vb%d" % g, [P, O], F32)
+            nc.scalar.activation(out=vb[:], in_=rows["q", g][:].indirect(l5[:]), func=ACT.Copy, scale=vec["so2"][:, col])
+            t1 = tile("t1%d" % g, [P, O], F32)
+            nc.vector.tensor_tensor(t1[:], va[:], g1[:], ALU.mult)
+            t2 = tile("t2%d" % g, [P, O], F32)
+            nc.vector.tensor_tensor(t2[:], vb[:], g2[:], ALU.mult)
+            y = tile("y%d" % g, [P, O], F32)
+            nc.vector.tensor_tensor(y[:], t1[:], t2[:], ALU.subtract)
+            nc.sync.dma_start(out[g * P : (g + 1) * P, :], y[:])

@@ -29,8 +29,8 @@ def tile_list_outcomegatedcross_twotab_kernel(
         sb = ctx.enter_context(tc.tile_pool(name="sb", bufs=1))
         ps = ctx.enter_context(tc.psum_pool(name="ps", bufs=1))
 
-        def tile(name, shape, dt):
-            return sb.tile(shape, dt, name=name, align_bytes=64)
+        def tile(name, shape, dt, tag=None):
+            return sb.tile(shape, dt, name=name, tag=tag or name, align_bytes=64)
 
         def words32(ap):
             return ap[0].rearrange("p n t -> p (n t)").bitcast(I32)
@@ -40,13 +40,13 @@ def tile_list_outcomegatedcross_twotab_kernel(
 
         xts_win = tile("xts_win", [P, T], U8)
         xos_win = tile("xos_win", [P, Z], U8)
-        w_raw_sc = tile("w_raw_sc", [P, 2 * R], U8)
-        out_sc = tile("out_sc", [P, 2 * N], U8)
-        for t in (xts_win, xos_win, w_raw_sc, out_sc):
-            nc.vector.memset(t[:].bitcast(I32), 0)
+        w_raw_sc = tile("w_raw_sc", [P, R], U8)
+        w2_raw_sc = tile("w2_raw_sc", [P, R], U8)
+        w_stage = tile("w_stage", [4, 4, R // 4], I32)
+        out_sc = tile("out_sc", [P, 4 * N], U8)
+        for ap in (xts_win[:], w2_raw_sc[:], xos_win[:], w_raw_sc[:], out_sc[:, 0 : 2 * N]):
+            nc.vector.memset(ap.bitcast(I32), 0)
 
-        st1 = tile("st1", [4, 4, 2 * R // 4], I32)
-        st2 = tile("st2", [4, 4, 2 * N // 4], I32)
         xtw = tile("xtw", [P, T], U16)
         xow = tile("xow", [P, Z], U32)
         ww = tile("ww", [P, R], U32)
@@ -60,20 +60,25 @@ def tile_list_outcomegatedcross_twotab_kernel(
         l5 = tile("l5", [P, O // 16], U16)
         l6 = tile("l6", [P, O // 16], U16)
 
+        def load_plane(win, scales):
+            for q in range(4):
+                nc.sync.dma_start(win[32 * q : 32 * q + 4, :].bitcast(I32), scales[0, 4 * q : 4 * q + 4, :].bitcast(I32))
+
         nc.gpsimd.dma_start(xtw[:].bitcast(I32), xt_words[0].bitcast(I32))
         nc.gpsimd.dma_start(xow[:].bitcast(I32), words32(xo_words))
-        nc.sync.dma_start(st1[:, :, 0 : R // 4], by_quadrant(w_scales))
-        nc.sync.dma_start(st1[:, :, R // 4 : R // 2], by_quadrant(w2_scales))
-        nc.sync.dma_start(l1[:], offs)
+        nc.gpsimd.dma_start(w2w[:].bitcast(I32), w2_words[0].bitcast(I32))
         nc.sync.dma_start(ww[:].bitcast(I32), words32(w_words))
-        for q in range(4):
-            nc.sync.dma_start(xts_win[32 * q : 32 * q + 4, :].bitcast(I32), xt_scales[0, 4 * q : 4 * q + 4, :].bitcast(I32))
+        nc.sync.dma_start(w_stage[:], by_quadrant(w_scales))
+        nc.sync.dma_start(l1[:], offs)
         nc.sync.dma_start(l2[:], offs2)
-        nc.sync.dma_start(w2w[:].bitcast(I32), w2_words[0].bitcast(I32))
-        for q in range(4):
-            nc.sync.dma_start(xos_win[32 * q : 32 * q + 4, :].bitcast(I32), xo_scales[0, 4 * q : 4 * q + 4, :].bitcast(I32))
-        nc.sync.dma_start(st2[:, :, 0 : N // 4], by_quadrant(wb_scales))
-        nc.sync.dma_start(st2[:, :, N // 4 : N // 2], by_quadrant(wc_scales))
+        load_plane(xts_win, xt_scales)
+        load_plane(w2_raw_sc, w2_scales)
+        load_plane(xos_win, xo_scales)
+        out_words = out_sc[:].bitcast(I32).rearrange("p (q c) -> p q c", q=2)
+        for i, scales in enumerate((wb_scales, wc_scales)):
+            for u in range(2):
+                nc.sync.dma_start(out_words[64 * u : 64 * u + 4, :, i * N // 4 : (i + 1) * N // 4],
+                                  by_quadrant(scales)[:, 2 * u : 2 * u + 2, :])
         nc.sync.dma_start(wbw[:].bitcast(I32), wb_words[0].bitcast(I32))
         nc.sync.dma_start(wcw[:].bitcast(I32), words32(wc_words))
         vec = {}
@@ -87,86 +92,85 @@ def tile_list_outcomegatedcross_twotab_kernel(
         load_vec(nc.sync, "sp2", sp2)
         load_vec(nc.sync, "bo2", bo2)
         nc.sync.dma_start(l3[:], offs3)
+        load_vec(nc.sync, "so", so)
         nc.sync.dma_start(l4[:], offs4)
+        load_vec(nc.sync, "sp", sp)
+        load_vec(nc.sync, "bo", bo)
         nc.sync.dma_start(l5[:], offs5)
-        load_vec(nc.gpsimd, "so", so)
-        load_vec(nc.gpsimd, "sp", sp)
-        load_vec(nc.gpsimd, "bo", bo)
-        load_vec(nc.gpsimd, "so2", so2)
+        load_vec(nc.sync, "so2", so2)
 
         for q in range(4):
-            nc.vector.tensor_copy(w_raw_sc[32 * q : 32 * q + 4, :].bitcast(I32), st1[:, q, :])
-        w_sc = tile("w_sc", [P, 2, 4, P], U8)
-        nc.vector.tensor_copy(w_sc[:], w_raw_sc[:].rearrange("p (w m t) -> p w t m", w=2, t=4))
-
+            nc.vector.tensor_copy(w_raw_sc[32 * q : 32 * q + 4, :].bitcast(I32), w_stage[:, q, :])
+        w_sc = tile("w_sc", [P, 4, P], U8)
+        nc.vector.tensor_copy(w_sc[:], w_raw_sc[:].rearrange("p (m t) -> p t m", t=4))
         xts = tile("xts", [P, J], U8)
         nc.vector.tensor_copy(xts[:], xts_win[:].indirect(l1[:]))
         xtg = tile("xtg", [P, J], U16)
         nc.vector.tensor_copy(xtg[:], xtw[:].indirect(l1[:]))
-        xos = tile("xos", [P, J], U8)
-        nc.vector.tensor_copy(xos[:], xos_win[:].indirect(l2[:]))
-        xog = []
+        xog = tile("xog", [P, J], U32)
+        nc.vector.tensor_copy(xog[:], xow[:].indirect(l2[:]))
+        w2_sc = tile("w2_sc", [P, 4, P], U8)
+        nc.vector.tensor_copy(w2_sc[:], w2_raw_sc[:].rearrange("p (m t) -> p t m", t=4))
+        xos = []
         for h in range(2):
-            g = tile("xog%d" % h, [P, P], U32)
-            nc.vector.tensor_copy(g[:], xow[:].indirect(l2[:, 8 * h : 8 * h + 8]))
-            xog.append(g)
+            g = tile("xos%d" % h, [P, P], U8)
+            nc.vector.tensor_copy(g[:], xos_win[:].indirect(l2[:, 8 * h : 8 * h + 8]))
+            xos.append(g)
 
         wp = tile("wp", [P, R], U32)
         nc.scalar.copy(wp[:].rearrange("p (t c i) -> p c t i", t=4, i=4), ww[:].rearrange("p (c i t) -> p c t i", t=4, i=4))
         w2p = tile("w2p", [P, R], U16)
         nc.scalar.copy(w2p[:].rearrange("p (t m) -> p t m", t=4), w2w[:].rearrange("p (m t) -> p t m", t=4))
 
+        a_all = tile("a_all", [P, 2, P, 4], F32, tag="w2w")
         a_sb = []
         for h in range(2):
             a_ps = ps.tile([P, 4, P], F32, name="a%d" % h)
             for t in range(4):
                 nc.tensor.matmul_mx(
                     out=a_ps[:, t, :],
-                    lhsT=wp[:, t * P : (t + 1) * P].bitcast(E4M3), lhsT_scale=w_sc[:, 0, t, :],
+                    lhsT=wp[:, t * P : (t + 1) * P].bitcast(E4M3), lhsT_scale=w_sc[:, t, :],
                     rhs=xtg[:, h * P : (h + 1) * P].bitcast(E2M1), rhs_scale=xts[:, h * P : (h + 1) * P],
                     start=True, stop=True,
                 )
-            s = tile("a_sb%d" % h, [P, P, 4], F32)
-            nc.scalar.copy(s[:], a_ps[:].rearrange("p t j -> p j t"))
+            s = a_all[:, h]
+            nc.scalar.copy(s, a_ps[:].rearrange("p t j -> p j t"))
             a_sb.append(s)
 
-        hid = []
+        hid = tile("hid", [P, J, 4], BF16)
         for h in range(2):
             b_ps = ps.tile([P, 4, P], F32, name="b%d" % h)
             for t in range(4):
                 nc.tensor.matmul_mx(
                     out=b_ps[:, t, :],
-                    lhsT=w2p[:, t * P : (t + 1) * P].bitcast(E2M1), lhsT_scale=w_sc[:, 1, t, :],
-                    rhs=xog[h][:].bitcast(E4M3), rhs_scale=xos[:, h * P : (h + 1) * P],
+                    lhsT=w2p[:, t * P : (t + 1) * P].bitcast(E2M1), lhsT_scale=w2_sc[:, t, :],
+                    rhs=xog[:, h * P : (h + 1) * P].bitcast(E4M3), rhs_scale=xos[h][:],
                     start=True, stop=True,
                 )
-            s = tile("hid%d" % h, [P, P, 4], BF16)
             if h == 0:
-                for q in range(4):
-                    nc.vector.tensor_copy(out_sc[32 * q : 32 * q + 4, :].bitcast(I32), st2[:, q, :])
-            nc.vector.tensor_tensor(s[:], b_ps[:].rearrange("p t j -> p j t"), a_sb[h][:], ALU.max)
-            hid.append(s)
+                for u in range(2):
+                    nc.vector.tensor_copy(out_words[64 * u + 32 : 64 * u + 36, 0, :], out_words[64 * u : 64 * u + 4, 1, :])
+            nc.vector.tensor_tensor(hid[:, h * P : (h + 1) * P, :], b_ps[:].rearrange("p t j -> p j t"), a_sb[h], ALU.max)
 
         hq = tile("hq", [P, J], U32)
         hs = tile("hs", [P, J], U8)
-        for h in range(2):
-            nc.vector.quantize_mx(
-                out=hq[:, h * P : (h + 1) * P].bitcast(E5M2), scales=hs[:, h * P : (h + 1) * P],
-                in_=hid[h][:].rearrange("p j t -> p (j t)"),
-            )
+        nc.vector.quantize_mx(out=hq[:].bitcast(E5M2), scales=hs[:], in_=hid[:].rearrange("p j t -> p (j t)"))
 
         rows = {}
         for g in range(2):
             for name, wt, fmt, c0 in (("p", wbw, E2M1, 0), ("q", wcw, E5M2, N)):
-                acc = ps.tile([P, J], F32, name="%s%d_ps" % (name, g))
-                nc.tensor.matmul_mx(
-                    out=acc[:],
-                    lhsT=wt[:, g * P : (g + 1) * P].bitcast(fmt), lhsT_scale=out_sc[:, c0 + g * P : c0 + (g + 1) * P],
-                    rhs=hq[:].bitcast(E5M2), rhs_scale=hs[:],
-                    start=True, stop=True,
-                )
                 s = tile("%s%d" % (name, g), [P, J], F32)
-                nc.vector.tensor_copy(s[:], acc[:])
+                first = False
+                for i, cols in enumerate((slice(0, P), slice(P, J)) if first else (slice(0, J),)):
+                    early = first and i == 0
+                    acc = ps.tile([P, cols.stop - cols.start], F32, name="%s%d_ps%d" % (name, g, i), tag="a0" if early else "%s%d" % (name, g))
+                    nc.tensor.matmul_mx(
+                        out=acc[:],
+                        lhsT=wt[:, g * P : (g + 1) * P].bitcast(fmt), lhsT_scale=out_sc[:, c0 + g * P : c0 + (g + 1) * P],
+                        rhs=hq[:, cols].bitcast(E5M2), rhs_scale=hs[:, cols],
+                        start=True, stop=True,
+                    )
+                    nc.vector.tensor_copy(s[:, cols], acc[:])
                 rows[name, g] = s
 
         for g in range(2):

@@ -27,6 +27,7 @@ def tile_list_outcomegatedcross_twotab_kernel(
     nc = tc.nc
     with ExitStack() as ctx:
         sb = ctx.enter_context(tc.tile_pool(name="sb", bufs=1))
+        late = ctx.enter_context(tc.tile_pool(name="late", bufs=1))
         ps = ctx.enter_context(tc.psum_pool(name="ps", bufs=1))
 
         def tile(name, shape, dt, tag=None):
@@ -40,19 +41,21 @@ def tile_list_outcomegatedcross_twotab_kernel(
 
         xts_win = tile("xts_win", [P, T], U8)
         xos_win = tile("xos_win", [P, Z], U8)
-        w_raw_sc = tile("w_raw_sc", [P, R], U8)
-        w2_raw_sc = tile("w2_raw_sc", [P, R], U8)
-        w_stage = tile("w_stage", [4, 4, R // 4], I32)
-        out_sc = tile("out_sc", [P, 4 * N], U8)
-        for ap in (xts_win[:], w2_raw_sc[:], xos_win[:], w_raw_sc[:], out_sc[:, 0 : 2 * N]):
+        w_raw_sc = tile("w_raw_sc", [P, 2 * R], U8)
+        out_sc = tile("out_sc", [P, 8 * N], U8)
+        for ap in (xts_win[:], xos_win[:], out_sc[:, 0 : 2 * N], w_raw_sc[:]):
             nc.vector.memset(ap.bitcast(I32), 0)
 
+        def placed(name, shape, dt, offset):
+            return late.tile(shape, dt, name=name, align_bytes=64, offset=offset)
+
+        w_stage = tile("w_stage", [4, 4, 2 * R // 4], I32)
         xtw = tile("xtw", [P, T], U16)
         xow = tile("xow", [P, Z], U32)
-        ww = tile("ww", [P, R], U32)
+        ww = placed("ww", [P, R], U32, 0)
         w2w = tile("w2w", [P, R], U16)
-        wbw = tile("wbw", [P, N], U16)
-        wcw = tile("wcw", [P, N], U32)
+        wbw = placed("wbw", [P, N], U16, 0)
+        wcw = placed("wcw", [P, N], U32, 512)
         l1 = tile("l1", [P, J // 16], U16)
         l2 = tile("l2", [P, J // 16], U16)
         l3 = tile("l3", [P, O // 16], U16)
@@ -66,25 +69,23 @@ def tile_list_outcomegatedcross_twotab_kernel(
 
         nc.gpsimd.dma_start(xtw[:].bitcast(I32), xt_words[0].bitcast(I32))
         nc.gpsimd.dma_start(xow[:].bitcast(I32), words32(xo_words))
-        nc.gpsimd.dma_start(w2w[:].bitcast(I32), w2_words[0].bitcast(I32))
-        nc.sync.dma_start(ww[:].bitcast(I32), words32(w_words))
-        nc.sync.dma_start(w_stage[:], by_quadrant(w_scales))
+        nc.sync.dma_start(w_stage[:, :, 0 : R // 4], by_quadrant(w_scales))
+        nc.sync.dma_start(w_stage[:, :, R // 4 : R // 2], by_quadrant(w2_scales))
         nc.sync.dma_start(l1[:], offs)
         nc.sync.dma_start(l2[:], offs2)
         load_plane(xts_win, xt_scales)
-        load_plane(w2_raw_sc, w2_scales)
+        nc.sync.dma_start(ww[:].bitcast(I32), words32(w_words))
+        nc.sync.dma_start(w2w[:].bitcast(I32), w2_words[0].bitcast(I32))
         load_plane(xos_win, xo_scales)
-        out_words = out_sc[:].bitcast(I32).rearrange("p (q c) -> p q c", q=2)
+        out_words = out_sc[:].bitcast(I32).rearrange("p (q c) -> p q c", q=4)
         for i, scales in enumerate((wb_scales, wc_scales)):
-            for u in range(2):
-                nc.sync.dma_start(out_words[64 * u : 64 * u + 4, :, i * N // 4 : (i + 1) * N // 4],
-                                  by_quadrant(scales)[:, 2 * u : 2 * u + 2, :])
+            nc.sync.dma_start(out_words[0:4, :, i * N // 4 : (i + 1) * N // 4], by_quadrant(scales))
         nc.sync.dma_start(wbw[:].bitcast(I32), wb_words[0].bitcast(I32))
         nc.sync.dma_start(wcw[:].bitcast(I32), words32(wc_words))
         vec = {}
 
         def load_vec(eng, name, ap):
-            vec[name] = tile("v_" + name, [P, 2], F32)
+            vec[name] = late.tile([P, 2], F32, name="v_" + name, align_bytes=64, offset=1536 + 64 * len(vec))
             with nc.allow_non_contiguous_dma(reason="one value a partition"):
                 eng.dma_start(vec[name][:], ap.rearrange("(h p) o -> p (h o)", p=P))
 
@@ -101,21 +102,17 @@ def tile_list_outcomegatedcross_twotab_kernel(
 
         for q in range(4):
             nc.vector.tensor_copy(w_raw_sc[32 * q : 32 * q + 4, :].bitcast(I32), w_stage[:, q, :])
-        w_sc = tile("w_sc", [P, 4, P], U8)
-        nc.vector.tensor_copy(w_sc[:], w_raw_sc[:].rearrange("p (m t) -> p t m", t=4))
+        w_sc = tile("w_sc", [P, 2, 4, P], U8)
+        nc.vector.tensor_copy(w_sc[:], w_raw_sc[:].rearrange("p (w m t) -> p w t m", w=2, t=4))
         xts = tile("xts", [P, J], U8)
         nc.vector.tensor_copy(xts[:], xts_win[:].indirect(l1[:]))
-        xtg = tile("xtg", [P, J], U16)
+        xtg = tile("xtg", [P, J], U16, tag="xts_win")
         nc.vector.tensor_copy(xtg[:], xtw[:].indirect(l1[:]))
-        xog = tile("xog", [P, J], U32)
-        nc.vector.tensor_copy(xog[:], xow[:].indirect(l2[:]))
-        w2_sc = tile("w2_sc", [P, 4, P], U8)
-        nc.vector.tensor_copy(w2_sc[:], w2_raw_sc[:].rearrange("p (m t) -> p t m", t=4))
-        xos = []
+        xos = tile("xos", [P, J], U8, tag="xtw")
+        nc.vector.tensor_copy(xos[:], xos_win[:].indirect(l2[:]))
+        xog = tile("xog", [P, J], U32, tag="xos_win")
         for h in range(2):
-            g = tile("xos%d" % h, [P, P], U8)
-            nc.vector.tensor_copy(g[:], xos_win[:].indirect(l2[:, 8 * h : 8 * h + 8]))
-            xos.append(g)
+            nc.vector.tensor_copy(xog[:, h * P : (h + 1) * P], xow[:].indirect(l2[:, 8 * h : 8 * h + 8]))
 
         wp = tile("wp", [P, R], U32)
         nc.scalar.copy(wp[:].rearrange("p (t c i) -> p c t i", t=4, i=4), ww[:].rearrange("p (c i t) -> p c t i", t=4, i=4))
@@ -129,7 +126,7 @@ def tile_list_outcomegatedcross_twotab_kernel(
             for t in range(4):
                 nc.tensor.matmul_mx(
                     out=a_ps[:, t, :],
-                    lhsT=wp[:, t * P : (t + 1) * P].bitcast(E4M3), lhsT_scale=w_sc[:, t, :],
+                    lhsT=wp[:, t * P : (t + 1) * P].bitcast(E4M3), lhsT_scale=w_sc[:, 0, t, :],
                     rhs=xtg[:, h * P : (h + 1) * P].bitcast(E2M1), rhs_scale=xts[:, h * P : (h + 1) * P],
                     start=True, stop=True,
                 )
@@ -143,18 +140,20 @@ def tile_list_outcomegatedcross_twotab_kernel(
             for t in range(4):
                 nc.tensor.matmul_mx(
                     out=b_ps[:, t, :],
-                    lhsT=w2p[:, t * P : (t + 1) * P].bitcast(E2M1), lhsT_scale=w2_sc[:, t, :],
-                    rhs=xog[:, h * P : (h + 1) * P].bitcast(E4M3), rhs_scale=xos[h][:],
+                    lhsT=w2p[:, t * P : (t + 1) * P].bitcast(E2M1), lhsT_scale=w_sc[:, 1, t, :],
+                    rhs=xog[:, h * P : (h + 1) * P].bitcast(E4M3), rhs_scale=xos[:, h * P : (h + 1) * P],
                     start=True, stop=True,
                 )
             if h == 0:
-                for u in range(2):
-                    nc.vector.tensor_copy(out_words[64 * u + 32 : 64 * u + 36, 0, :], out_words[64 * u : 64 * u + 4, 1, :])
+                for q in range(1, 4):
+                    nc.vector.tensor_copy(out_words[32 * q : 32 * q + 4, 0, :], out_words[0:4, q, :])
             nc.vector.tensor_tensor(hid[:, h * P : (h + 1) * P, :], b_ps[:].rearrange("p t j -> p j t"), a_sb[h], ALU.max)
 
         hq = tile("hq", [P, J], U32)
         hs = tile("hs", [P, J], U8)
-        nc.vector.quantize_mx(out=hq[:].bitcast(E5M2), scales=hs[:], in_=hid[:].rearrange("p j t -> p (j t)"))
+        for h in range(2):
+            cols = slice(h * P, (h + 1) * P)
+            nc.vector.quantize_mx(out=hq[:, cols].bitcast(E5M2), scales=hs[:, cols], in_=hid[:, cols, :].rearrange("p j t -> p (j t)"))
 
         rows = {}
         for g in range(2):

from contextlib import ExitStack

import concourse.mybir as mybir

F32 = mybir.dt.float32
BF16 = mybir.dt.bfloat16
I32 = mybir.dt.int32
U32 = mybir.dt.uint32
U16 = mybir.dt.uint16
U8 = mybir.dt.uint8
E4M3 = mybir.dt.float8_e4m3fn_x4
E5M2 = mybir.dt.float8_e5m2_x4
E2M1 = mybir.dt.float4_e2m1fn_x4
ACT = mybir.ActivationFunctionType
ALU = mybir.AluOpType

P = 128
K, T, J, R, F, Z, N, O = 512, 1024, 256, 512, 512, 1024, 256, 128
FLOPS = 2 * K * R * J + 2 * F * R * J + 2 * 2 * R * N * J


def tile_list_outcomegatedcross_twotab_kernel(
    tc, xt_words, xt_scales, xo_words, xo_scales, w_words, w_scales, w2_words, w2_scales,
    wb_words, wb_scales, wc_words, wc_scales, so, sp, bo, so2, sp2, bo2,
    offs, offs2, offs3, offs4, offs5, offs6, out,
):
    nc = tc.nc
    with ExitStack() as ctx:
        sb = ctx.enter_context(tc.tile_pool(name="sb", bufs=1))
        late = ctx.enter_context(tc.tile_pool(name="late", bufs=1))
        ps = ctx.enter_context(tc.psum_pool(name="ps", bufs=1))

        def tile(name, shape, dt, tag=None):
            return sb.tile(shape, dt, name=name, tag=tag or name, align_bytes=64)

        def words32(ap):
            return ap[0].rearrange("p n t -> p (n t)").bitcast(I32)

        def by_quadrant(ap):
            return ap[0].bitcast(I32).rearrange("(q r) c -> r q c", r=4)

        xts_win = tile("xts_win", [P, T], U8)
        xos_win = tile("xos_win", [P, Z], U8)
        w_raw_sc = tile("w_raw_sc", [P, 2 * R], U8)
        out_sc = tile("out_sc", [P, 8 * N], U8)
        for ap in (xts_win[:], xos_win[:], out_sc[:, 0 : 2 * N], w_raw_sc[:]):
            nc.vector.memset(ap.bitcast(I32), 0)

        def placed(name, shape, dt, offset):
            return late.tile(shape, dt, name=name, align_bytes=64, offset=offset)

        w_stage = tile("w_stage", [4, 4, 2 * R // 4], I32)
        xtw = tile("xtw", [P, T], U16)
        xow = tile("xow", [P, Z], U32)
        ww = placed("ww", [P, R], U32, 0)
        w2w = tile("w2w", [P, R], U16)
        wbw = placed("wbw", [P, N], U16, 0)
        wcw = placed("wcw", [P, N], U32, 512)
        l1 = tile("l1", [P, J // 16], U16)
        l2 = tile("l2", [P, J // 16], U16)
        l3 = tile("l3", [P, O // 16], U16)
        l4 = tile("l4", [P, O // 16], U16)
        l5 = tile("l5", [P, O // 16], U16)
        l6 = tile("l6", [P, O // 16], U16)

        def load_plane(win, scales):
            for q in range(4):
                nc.sync.dma_start(win[32 * q : 32 * q + 4, :].bitcast(I32), scales[0, 4 * q : 4 * q + 4, :].bitcast(I32))

        nc.gpsimd.dma_start(xtw[:].bitcast(I32), xt_words[0].bitcast(I32))
        nc.gpsimd.dma_start(xow[:].bitcast(I32), words32(xo_words))
        nc.sync.dma_start(w_stage[:, :, 0 : R // 4], by_quadrant(w_scales))
        nc.sync.dma_start(w_stage[:, :, R // 4 : R // 2], by_quadrant(w2_scales))
        nc.sync.dma_start(l1[:], offs)
        nc.sync.dma_start(l2[:], offs2)
        load_plane(xts_win, xt_scales)
        nc.sync.dma_start(ww[:].bitcast(I32), words32(w_words))
        nc.sync.dma_start(w2w[:].bitcast(I32), w2_words[0].bitcast(I32))
        load_plane(xos_win, xo_scales)
        out_words = out_sc[:].bitcast(I32).rearrange("p (q c) -> p q c", q=4)
        for i, scales in enumerate((wb_scales, wc_scales)):
            nc.sync.dma_start(out_words[0:4, :, i * N // 4 : (i + 1) * N // 4], by_quadrant(scales))
        nc.sync.dma_start(wbw[:].bitcast(I32), wb_words[0].bitcast(I32))
        nc.sync.dma_start(wcw[:].bitcast(I32), words32(wc_words))
        vec = {}

        def load_vec(eng, name, ap):
            vec[name] = late.tile([P, 2], F32, name="v_" + name, align_bytes=64, offset=1536 + 64 * len(vec))
            with nc.allow_non_contiguous_dma(reason="one value a partition"):
                eng.dma_start(vec[name][:], ap.rearrange("(h p) o -> p (h o)", p=P))

        nc.sync.dma_start(l6[:], offs6)
        load_vec(nc.sync, "sp2", sp2)
        load_vec(nc.sync, "bo2", bo2)
        nc.sync.dma_start(l3[:], offs3)
        load_vec(nc.sync, "so", so)
        nc.sync.dma_start(l4[:], offs4)
        load_vec(nc.sync, "sp", sp)
        load_vec(nc.sync, "bo", bo)
        nc.sync.dma_start(l5[:], offs5)
        load_vec(nc.sync, "so2", so2)

        for q in range(4):
            nc.vector.tensor_copy(w_raw_sc[32 * q : 32 * q + 4, :].bitcast(I32), w_stage[:, q, :])
        w_sc = tile("w_sc", [P, 2, 4, P], U8)
        nc.vector.tensor_copy(w_sc[:], w_raw_sc[:].rearrange("p (w m t) -> p w t m", w=2, t=4))
        xts = tile("xts", [P, J], U8)
        nc.vector.tensor_copy(xts[:], xts_win[:].indirect(l1[:]))
        xtg = tile("xtg", [P, J], U16, tag="xts_win")
        nc.vector.tensor_copy(xtg[:], xtw[:].indirect(l1[:]))
        xos = tile("xos", [P, J], U8, tag="xtw")
        nc.vector.tensor_copy(xos[:], xos_win[:].indirect(l2[:]))
        xog = tile("xog", [P, J], U32, tag="xos_win")
        for h in range(2):
            nc.vector.tensor_copy(xog[:, h * P : (h + 1) * P], xow[:].indirect(l2[:, 8 * h : 8 * h + 8]))

        wp = tile("wp", [P, R], U32)
        nc.scalar.copy(wp[:].rearrange("p (t c i) -> p c t i", t=4, i=4), ww[:].rearrange("p (c i t) -> p c t i", t=4, i=4))
        w2p = tile("w2p", [P, R], U16)
        nc.scalar.copy(w2p[:].rearrange("p (t m) -> p t m", t=4), w2w[:].rearrange("p (m t) -> p t m", t=4))

        a_all = tile("a_all", [P, 2, P, 4], F32, tag="w2w")
        a_sb = []
        for h in range(2):
            a_ps = ps.tile([P, 4, P], F32, name="a%d" % h)
            for t in range(4):
                nc.tensor.matmul_mx(
                    out=a_ps[:, t, :],
                    lhsT=wp[:, t * P : (t + 1) * P].bitcast(E4M3), lhsT_scale=w_sc[:, 0, t, :],
                    rhs=xtg[:, h * P : (h + 1) * P].bitcast(E2M1), rhs_scale=xts[:, h * P : (h + 1) * P],
                    start=True, stop=True,
                )
            s = a_all[:, h]
            nc.scalar.copy(s, a_ps[:].rearrange("p t j -> p j t"))
            a_sb.append(s)

        hid = tile("hid", [P, J, 4], BF16)
        for h in range(2):
            b_ps = ps.tile([P, 4, P], F32, name="b%d" % h)
            for t in range(4):
                nc.tensor.matmul_mx(
                    out=b_ps[:, t, :],
                    lhsT=w2p[:, t * P : (t + 1) * P].bitcast(E2M1), lhsT_scale=w_sc[:, 1, t, :],
                    rhs=xog[:, h * P : (h + 1) * P].bitcast(E4M3), rhs_scale=xos[:, h * P : (h + 1) * P],
                    start=True, stop=True,
                )
            if h == 0:
                for q in range(1, 4):
                    nc.vector.tensor_copy(out_words[32 * q : 32 * q + 4, 0, :], out_words[0:4, q, :])
            nc.vector.tensor_tensor(hid[:, h * P : (h + 1) * P, :], b_ps[:].rearrange("p t j -> p j t"), a_sb[h], ALU.max)

        hq = tile("hq", [P, J], U32)
        hs = tile("hs", [P, J], U8)
        for h in range(2):
            cols = slice(h * P, (h + 1) * P)
            nc.vector.quantize_mx(out=hq[:, cols].bitcast(E5M2), scales=hs[:, cols], in_=hid[:, cols, :].rearrange("p j t -> p (j t)"))

        rows = {}
        for g in range(2):
            for name, wt, fmt, c0 in (("p", wbw, E2M1, 0), ("q", wcw, E5M2, N)):
                s = tile("%s%d" % (name, g), [P, J], F32)
                first = False
                for i, cols in enumerate((slice(0, P), slice(P, J)) if first else (slice(0, J),)):
                    early = first and i == 0
                    acc = ps.tile([P, cols.stop - cols.start], F32, name="%s%d_ps%d" % (name, g, i), tag="a0" if early else "%s%d" % (name, g))
                    nc.tensor.matmul_mx(
                        out=acc[:],
                        lhsT=wt[:, g * P : (g + 1) * P].bitcast(fmt), lhsT_scale=out_sc[:, c0 + g * P : c0 + (g + 1) * P],
                        rhs=hq[:, cols].bitcast(E5M2), rhs_scale=hs[:, cols],
                        start=True, stop=True,
                    )
                    nc.vector.tensor_copy(s[:, cols], acc[:])
                rows[name, g] = s

        for g in range(2):
            col = slice(g, g + 1)
            g2 = tile("g2%d" % g, [P, O], F32)
            nc.scalar.activation(out=g2[:], in_=rows["p", g][:].indirect(l6[:]), func=ACT.Sigmoid,
                                 bias=vec["bo2"][:, col], scale=vec["sp2"][:, col])
            va = tile("va%d" % g, [P, O], F32)
            nc.scalar.activation(out=va[:], in_=rows["p", g][:].indirect(l3[:]), func=ACT.Copy, scale=vec["so"][:, col])
            g1 = tile("g1%d" % g, [P, O], F32)
            nc.scalar.activation(out=g1[:], in_=rows["q", g][:].indirect(l4[:]), func=ACT.Sigmoid,
                                 bias=vec["bo"][:, col], scale=vec["sp"][:, col])
            vb = tile("vb%d" % g, [P, O], F32)
            nc.scalar.activation(out=vb[:], in_=rows["q", g][:].indirect(l5[:]), func=ACT.Copy, scale=vec["so2"][:, col])
            t1 = tile("t1%d" % g, [P, O], F32)
            nc.vector.tensor_tensor(t1[:], va[:], g1[:], ALU.mult)
            t2 = tile("t2%d" % g, [P, O], F32)
            nc.vector.tensor_tensor(t2[:], vb[:], g2[:], ALU.mult)
            y = tile("y%d" % g, [P, O], F32)
            nc.vector.tensor_tensor(y[:], t1[:], t2[:], ALU.subtract)
            nc.sync.dma_start(out[g * P : (g + 1) * P, :], y[:])
